import numpy as np
import ml_dtypes


def mxq(x, axis, fmt="e4m3"):
    dtype, down = {"e4m3": (ml_dtypes.float8_e4m3fn, 7), "e5m2": (ml_dtypes.float8_e5m2, 14)}[fmt]
    v = np.moveaxis(np.asarray(x, np.float32).astype(ml_dtypes.bfloat16).astype(np.float64), axis, -1)
    blocks = v.reshape(v.shape[:-1] + (-1, 32))
    amax = np.abs(blocks).max(-1, keepdims=True)
    byte = np.maximum(np.where(amax > 0, np.frexp(amax)[1] - 1 + 127, 0) - down, 1)
    scale = np.exp2(byte - 127.0)
    codes = (blocks / scale).astype(np.float32).astype(dtype).astype(np.float64)
    return np.moveaxis((codes * scale).reshape(v.shape), -1, axis)


WIDE = False


def mx_kscale(k):
    if not WIDE:
        return np.ones(k)
    levels = np.array([10, -10, 5, -5, 0])
    if k % 512:
        return np.exp2(np.random.permutation(np.resize(levels, k // 32))).repeat(32)
    a = np.empty((k // 512, 16))
    for p in range(k // 512):
        a[p, :8] = np.random.permutation(np.resize(levels, 8))
        for g in range(8):
            far = levels[np.abs(levels - a[p, g]) >= 10]
            a[p, g + 8] = far[np.random.randint(len(far))]
    return np.exp2(a.ravel()).repeat(32)


def f64(x):
    return np.asarray(x).astype(np.float64)


def striped(idx):
    return np.tile(idx.reshape(-1, 16).T, (8, 1)).astype(np.uint16)


def unstriped(offs):
    return offs[:16].T.reshape(-1).astype(np.int64)


def striped8(idx):
    return np.concatenate([x.reshape(-1, 16).T for x in idx]).astype(np.uint16)


def runs(offs, k):
    lists = np.stack([offs[16 * r : 16 * r + 16].T.reshape(-1) for r in range(8)]).astype(np.int64)
    return lists[np.arange(k) % 512 // 64]


def pack_weight(w):
    k, n = w.shape
    w = f64(np.asarray(w, np.float32).astype(ml_dtypes.bfloat16)).reshape(k // 32, 32, n)
    amax = np.abs(w).max(1)
    byte = np.clip(np.where(amax > 0, np.frexp(amax)[1] - 1 + 127 - 7, 1), 1, 254)
    scaled = (w * np.exp2(127.0 - byte)[:, None, :]).reshape(k, n).astype(np.float32)
    words = np.ascontiguousarray(scaled.reshape(k // 512, 128, 4, n).transpose(0, 1, 3, 2)).astype(ml_dtypes.float8_e4m3fn).view(np.uint8)
    return words, np.ascontiguousarray(byte.astype(np.uint8).reshape(k // 512, 16, n))


def unpack_weight(words, scales):
    g, p, n, _ = words.shape
    vals = np.ascontiguousarray(words).view(ml_dtypes.float8_e4m3fn).astype(np.float64) * np.repeat(np.exp2(scales.astype(np.float64) - 127.0), 8, axis=1)[..., None]
    return vals.transpose(0, 1, 3, 2).reshape(g * 512, n)


def sigmoid(v):
    return 1.0 / (1.0 + np.exp(-np.maximum(v, -700.0)))

def planes(y):
    n, m = y.shape
    v = y.astype(np.float32).astype(ml_dtypes.bfloat16).astype(np.float64).reshape(n // 32, 32, m)
    top = np.abs(v).max(1)
    byte = np.clip(np.where(top > 0, np.frexp(top)[1] - 1 + 127 - 7, 1), 1, 254)
    codes = (v * np.exp2(127.0 - byte)[:, None, :]).reshape(n, m).astype(np.float32).astype(ml_dtypes.float8_e4m3fn).view(np.uint8)
    words = codes.reshape(n // 512, 128, 4, m).transpose(0, 1, 3, 2)
    return np.ascontiguousarray(words), np.ascontiguousarray(byte.astype(np.uint8).reshape(n // 512, 16, m))


K, T, S, H, G = 512, 2048, 512, 512, 2048


def setup_inputs():
    n = np.random.standard_normal
    s = mx_kscale(K)[:, None]
    packed_xT = pack_weight(n((K, T)) * s)
    packed_w1 = pack_weight(n((K, H)) / np.sqrt(K) / s)
    packed_w2 = pack_weight(n((K, H)) / np.sqrt(K) / s)
    packed_dT = pack_weight(n((K, G)) / s)
    return {
        "x_words": packed_xT[0],
        "x_scales": packed_xT[1],
        "w1_words": packed_w1[0],
        "w1_scales": packed_w1[1],
        "w2_words": packed_w2[0],
        "w2_scales": packed_w2[1],
        "gs": (np.random.uniform(0.5, 1.5, (K, 1)) * s).astype(np.float32),
        "d_words": packed_dT[0],
        "d_scales": packed_dT[1],
        "offs": striped(np.random.permutation(T)[:S]),
        "two": striped(np.random.permutation(T)[:S]),
        "la": striped8(np.stack([np.random.permutation(S) for _ in range(8)])),
        "lb": striped8(np.stack([np.random.permutation(S) for _ in range(8)])),
        "kq": striped8(np.random.randint(0, G, (8, H))),
    }


def reference(x_words, x_scales, w1_words, w1_scales, w2_words, w2_scales, gs, d_words, d_scales, offs, two, la, lb, kq):
    d_kq = unpack_weight(d_words, d_scales)[np.arange(K)[:, None], runs(kq, K)]
    xq = unpack_weight(x_words, x_scales)[:, unstriped(offs)]
    y = sigmoid(unpack_weight(w1_words, w1_scales).T @ xq)
    a = y[np.arange(H)[:, None], runs(la, H)]
    x_two = unpack_weight(x_words, x_scales)[:, unstriped(two)]
    c = sigmoid(unpack_weight(w2_words, w2_scales).T @ x_two)
    b = c[np.arange(H)[:, None], runs(lb, H)]
    m1 = a * b
    z = f64(gs) * (m1 / (m1 + 0.25 * (a - m1) + 0.75 * (b - m1)))
    out_0 = 0.0625 * ((d_kq.T @ mxq(z, 0, "e4m3")))
    return (out_0,) + planes(out_0)

@@ -1,0 +1,213 @@
+import math
+from contextlib import ExitStack
+
+import concourse.mybir as mybir
+
+F32 = mybir.dt.float32
+BF16 = mybir.dt.bfloat16
+I32 = mybir.dt.int32
+U32 = mybir.dt.uint32
+U16 = mybir.dt.uint16
+U8 = mybir.dt.uint8
+FP8X4 = mybir.dt.float8_e4m3fn_x4
+ACT = mybir.ActivationFunctionType
+ALU = mybir.AluOpType
+
+P = 128
+PACK = 4
+TABLE = 2048
+N = 512
+HALF = 256
+QUARTER = 128
+ON_SCALAR = 3
+SQUARE_ON_SCALAR = ( 1, 2, 3,)
+FLOPS = 3 * 2 * 512 * 512 * 512
+
+
+def tile_picked_tversky2_none_po_kernel(
+    tc, x_words, x_scales, w1_words, w1_scales, w2_words, w2_scales, gs, d_words, d_scales,
+    offs, two, la, lb, kq, out_0, out_1, out_2,
+):
+    nc = tc.nc
+    with ExitStack() as ctx:
+        keep = ctx.enter_context(tc.tile_pool(name="keep", bufs=1))
+        psum = ctx.enter_context(tc.psum_pool(name="psum", bufs=1))
+
+        def sb(name, shape, dtype, slot=None):
+            return keep.tile(shape, dtype, name=name, tag=slot or name, align_bytes=64)
+
+        def load_list(name, src):
+            tile = keep.tile([P, N // 16], U16, name=name)
+            nc.sync.dma_start(tile[:], src)
+            return tile
+
+        def load_words(name, src, width, queue):
+            tile = sb(name, [P, width], U32)
+            queue.dma_start(tile[:].bitcast(I32), src[0].rearrange("p n t -> p (n t)").bitcast(I32))
+            return tile
+
+        def zeroed_bytes(name, width):
+            tile = sb(name, [P, width], U8)
+            nc.vector.memset(tile[:].bitcast(I32), 0)
+            return tile
+
+        def load_scale_rows(tile, src, first, queue):
+            for q in range(4):
+                queue.dma_start(tile[32 * q + first : 32 * q + first + 4, :].bitcast(I32), src[0, 4 * q : 4 * q + 4, :].bitcast(I32))
+
+        def gather(name, dtype, table, offsets, slot=None):
+            tile = sb(name, [P, N], dtype, slot)
+            nc.vector.tensor_copy(tile[:], table[:].indirect(offsets[:]))
+            return tile
+
+        def deal(name, src, dtype, run, engine):
+            tile = sb(name, [P, N], src.dtype)
+            engine.tensor_copy(
+                tile[:].bitcast(dtype).rearrange("p (t c i) -> p c t i", t=PACK, i=run),
+                src[:].bitcast(dtype).rearrange("p (c i t) -> p c t i", t=PACK, i=run),
+            )
+            return tile
+
+        xs_table = zeroed_bytes("xs_table", TABLE)
+        w2s_raw = zeroed_bytes("w2s_raw", N)
+        w1s_raw = zeroed_bytes("w1s_raw", N)
+        ds_table = zeroed_bytes("ds_table", TABLE)
+
+        offs_t = load_list("offs_t", offs)
+        w1_raw = load_words("w1_raw", w1_words, N, nc.sync)
+        load_scale_rows(xs_table, x_scales, 0, nc.sync)
+        two_t = load_list("two_t", two)
+        xw_table = load_words("xw_table", x_words, TABLE, nc.sync)
+        load_scale_rows(w1s_raw, w1_scales, 0, nc.sync)
+        load_scale_rows(w2s_raw, w2_scales, 0, nc.gpsimd)
+        w2_raw = load_words("w2_raw", w2_words, N, nc.sync)
+        la_t = load_list("la_t", la)
+        dw_table = load_words("dw_table", d_words, TABLE, nc.sync)
+        kq_t = load_list("kq_t", kq)
+        for r in range(4):
+            home = r if r < 2 else 14 + r
+            nc.sync.dma_start(ds_table[home:P:32, :].bitcast(I32), d_scales[0, r:16:4, :].bitcast(I32))
+        lb_t = load_list("lb_t", lb)
+        gs_t = sb("gs_t", [P, PACK], F32)
+        nc.sync.dma_start(gs_t[:], gs.rearrange("(p t) o -> p (t o)", t=PACK))
+
+        w1 = deal("w1", w1_raw, I32, 4, nc.vector)
+        x1s = gather("x1s", U8, xs_table, offs_t)
+        x2s = gather("x2s", U8, xs_table, two_t)
+        x1w = gather("x1w", U32, xw_table, offs_t)
+        w1s = deal("w1s", w1s_raw, U8, 16, nc.vector)
+
+        def first_product(tag, w, ws, xw, xs):
+            banks = []
+            for t in range(PACK):
+                bank = psum.tile([P, N], F32, name="%s%d" % (tag, t), tag="%s%d" % (tag, t))
+                cols = slice(t * P, (t + 1) * P)
+                nc.tensor.matmul_mx(out=bank[:], lhsT=w[:, cols].bitcast(FP8X4), lhsT_scale=ws[:, cols],
+                                    rhs=xw[:].bitcast(FP8X4), rhs_scale=xs[:], start=True, stop=True)
+                banks.append(bank)
+            return banks
+
+        u_banks = first_product("bank_u", w1, w1s, x1w, x1s)
+        x2w = gather("x2w", U32, xw_table, two_t, "w1s_raw")
+        w2 = deal("w2", w2_raw, I32, 4, nc.gpsimd)
+        w2s = deal("w2s", w2s_raw, U8, 16, nc.gpsimd)
+        v_banks = first_product("bank_v", w2, w2s, x2w, x2s)
+
+        dw_picked = gather("dw_picked", U32, dw_table, kq_t)
+        ds_picked = gather("ds_picked", U8, ds_table, kq_t)
+        dw = deal("dw", dw_picked, I32, 4, nc.vector)
+        ds = deal("ds", ds_picked, U8, 16, nc.vector)
+        for r in (2, 3):
+            nc.sync.dma_start(ds[r:P:32, :].bitcast(I32), ds[14 + r:P:32, :].bitcast(I32))
+
+        u_rows = [sb("u_rows%d" % t, [P, N], F32) for t in range(PACK)]
+        ev_rows = [sb("ev_rows%d" % t, [P, N], F32) for t in range(PACK)]
+        eu = [[sb("eu%d%d" % (h, t), [P, HALF], F32, "ds_picked" if (h, t) == (0, ON_SCALAR) else None) for t in range(PACK)] for h in range(2)]
+        tot = [sb("tot%d" % h, [P, PACK, HALF], F32, None if h else "dw_picked") for h in range(2)]
+
+        def places(lst, h):
+            return lst[:, h * HALF // 16 : (h + 1) * HALF // 16]
+
+        def fetch_u(t, h):
+            if t < ON_SCALAR:
+                nc.scalar.activation(eu[h][t][:], u_rows[t][:].indirect(places(la_t, h)), ACT.Exp, scale=-1.0)
+            else:
+                nc.vector.tensor_copy(eu[h][t][:], u_rows[t][:].indirect(places(la_t, h)))
+
+        def fetch_v(t, h):
+            nc.vector.tensor_tensor(tot[h][:, t, :], ev_rows[t][:].indirect(places(lb_t, h)), eu[h][t][:], ALU.add)
+
+        for t in range(PACK):
+            if t < ON_SCALAR:
+                nc.scalar.activation(u_rows[t][:], u_banks[t][:], ACT.Copy)
+            else:
+                nc.scalar.activation(u_rows[t][:], u_banks[t][:], ACT.Exp, scale=-1.0)
+        for t in range(ON_SCALAR, PACK):
+            fetch_u(t, 0)
+        for t in range(PACK):
+            if t < ON_SCALAR:
+                fetch_u(t, 0)
+            nc.scalar.activation(ev_rows[t][:], v_banks[t][:], ACT.Exp, scale=-1.0, bias=-math.log(3.0))
+            fetch_v(t, 0)
+        for t in range(ON_SCALAR, PACK):
+            fetch_u(t, 1)
+        for t in range(PACK):
+            if t < ON_SCALAR:
+                fetch_u(t, 1)
+            fetch_v(t, 1)
+
+        z_words = sb("z_words", [P, N], U32)
+        z_scales = sb("z_scales", [P, N], U8)
+        y_words = sb("y_words", [P, N], U32)
+        y_scales = sb("y_scales", [P, N], U8)
+        out_rows = out_0.rearrange("(p t) j -> p t j", t=PACK)
+        words_out = out_1[0].rearrange("p n t -> p (n t)").bitcast(I32)
+
+        def woven(tile):
+            return tile[:].rearrange("p (c i) t -> p c t i", i=4)
+
+        def planes(tile):
+            return tile[:].rearrange("p t (c i) -> p c t i", i=4)
+
+        def flat(tile):
+            return tile[:].rearrange("p j t -> p (j t)")
+
+        def make_z(c):
+            cols = slice(c * QUARTER, (c + 1) * QUARTER)
+            root = sb("root%d" % c, [P, PACK, QUARTER], F32)
+            inv = sb("inv%d" % c, [P, PACK, QUARTER], F32)
+            z_bf = sb("z_bf%d" % c, [P, QUARTER, PACK], BF16)
+            nc.scalar.activation(root[:], tot[c // 2][:, :, (c % 2) * QUARTER : (c % 2 + 1) * QUARTER], ACT.Abs_reciprocal_sqrt, scale=0.75, bias=1.0)
+            if c in SQUARE_ON_SCALAR:
+                nc.scalar.activation(inv[:], root[:], ACT.Square)
+                nc.vector.tensor_tensor(woven(z_bf), planes(inv), gs_t[:].unsqueeze(1).unsqueeze(3).to_broadcast([P, QUARTER // 4, PACK, 4]), ALU.mult)
+            else:
+                for t in range(PACK):
+                    nc.vector.scalar_tensor_tensor(inv[:, t, :], root[:, t, :], gs_t[:, t : t + 1], root[:, t, :], ALU.mult, ALU.mult)
+                nc.vector.tensor_copy(woven(z_bf), planes(inv))
+            nc.vector.quantize_mx(z_words[:, cols].bitcast(FP8X4), z_scales[:, cols], flat(z_bf))
+
+        def make_y(c):
+            cols = slice(c * QUARTER, (c + 1) * QUARTER)
+            y = sb("y%d" % c, [P, PACK, QUARTER], F32)
+            y_bf = sb("y_bf%d" % c, [P, QUARTER, PACK], BF16)
+            bank = psum.tile([P, PACK, QUARTER], F32, name="bank_y%d" % c, tag="bank_u%d" % c)
+            for t in range(PACK):
+                rows = slice(t * P, (t + 1) * P)
+                nc.tensor.matmul_mx(out=bank[:, t, :], lhsT=dw[:, rows].bitcast(FP8X4), lhsT_scale=ds[:, rows],
+                                    rhs=z_words[:, cols].bitcast(FP8X4), rhs_scale=z_scales[:, cols], start=True, stop=True)
+            nc.scalar.activation(y[:], bank[:], ACT.Copy, scale=0.0625)
+            nc.sync.dma_start(out_rows[:, :, cols], y[:])
+            nc.vector.tensor_copy(woven(y_bf), planes(y))
+            nc.vector.quantize_mx(y_words[:, cols].bitcast(FP8X4), y_scales[:, cols], flat(y_bf))
+
+        for c in range(4):
+            make_z(c)
+        for c in range(4):
+            make_y(c)
+            if c == 1:
+                nc.sync.dma_start(words_out[:, :HALF], y_words[:, :HALF].bitcast(I32))
+        nc.sync.dma_start(words_out[:, HALF:], y_words[:, HALF:].bitcast(I32))
+        for q in range(4):
+            queue = nc.sync if q % 2 else nc.scalar
+            queue.dma_start(out_2[0, 4 * q : 4 * q + 4, :].bitcast(I32), y_scales[32 * q : 32 * q + 4, :].bitcast(I32))

@@ -20,7 +20,7 @@ N = 512
 HALF = 256
 QUARTER = 128
 ON_SCALAR = 3
-SQUARE_ON_SCALAR = ( 1, 2, 3,)
+SQUARE_ON_SCALAR = (  2, 3,)
 FLOPS = 3 * 2 * 512 * 512 * 512
 
 
@@ -46,14 +46,14 @@ def tile_picked_tversky2_none_po_kernel(
             queue.dma_start(tile[:].bitcast(I32), src[0].rearrange("p n t -> p (n t)").bitcast(I32))
             return tile
 
-        def zeroed_bytes(name, width):
+        def zeroed_bytes(name, width, engine):
             tile = sb(name, [P, width], U8)
-            nc.vector.memset(tile[:].bitcast(I32), 0)
+            engine.memset(tile[:].bitcast(I32), 0)
             return tile
 
-        def load_scale_rows(tile, src, first, queue):
-            for q in range(4):
-                queue.dma_start(tile[32 * q + first : 32 * q + first + 4, :].bitcast(I32), src[0, 4 * q : 4 * q + 4, :].bitcast(I32))
+        def load_scale_rows(tile, src, quadrants, queue):
+            for q in quadrants:
+                queue.dma_start(tile[32 * q : 32 * q + 4, :].bitcast(I32), src[0, 4 * q : 4 * q + 4, :].bitcast(I32))
 
         def gather(name, dtype, table, offsets, slot=None):
             tile = sb(name, [P, N], dtype, slot)
@@ -68,18 +68,18 @@ def tile_picked_tversky2_none_po_kernel(
             )
             return tile
 
-        xs_table = zeroed_bytes("xs_table", TABLE)
-        w2s_raw = zeroed_bytes("w2s_raw", N)
-        w1s_raw = zeroed_bytes("w1s_raw", N)
-        ds_table = zeroed_bytes("ds_table", TABLE)
+        xs_table = zeroed_bytes("xs_table", TABLE, nc.vector)
+        w2s_raw = zeroed_bytes("w2s_raw", N, nc.gpsimd)
+        w1s_raw = zeroed_bytes("w1s_raw", N, nc.vector)
+        ds_table = zeroed_bytes("ds_table", TABLE, nc.vector)
 
         offs_t = load_list("offs_t", offs)
         w1_raw = load_words("w1_raw", w1_words, N, nc.sync)
-        load_scale_rows(xs_table, x_scales, 0, nc.sync)
+        load_scale_rows(xs_table, x_scales, range(4), nc.sync)
         two_t = load_list("two_t", two)
         xw_table = load_words("xw_table", x_words, TABLE, nc.sync)
-        load_scale_rows(w1s_raw, w1_scales, 0, nc.sync)
-        load_scale_rows(w2s_raw, w2_scales, 0, nc.gpsimd)
+        load_scale_rows(w1s_raw, w1_scales, range(4), nc.sync)
+        load_scale_rows(w2s_raw, w2_scales, range(4), nc.gpsimd)
         w2_raw = load_words("w2_raw", w2_words, N, nc.sync)
         la_t = load_list("la_t", la)
         dw_table = load_words("dw_table", d_words, TABLE, nc.sync)
@@ -91,27 +91,36 @@ def tile_picked_tversky2_none_po_kernel(
         gs_t = sb("gs_t", [P, PACK], F32)
         nc.sync.dma_start(gs_t[:], gs.rearrange("(p t) o -> p (t o)", t=PACK))
 
+        def places(lst, h):
+            return lst[:, h * HALF // 16 : (h + 1) * HALF // 16]
+
         w1 = deal("w1", w1_raw, I32, 4, nc.vector)
         x1s = gather("x1s", U8, xs_table, offs_t)
         x2s = gather("x2s", U8, xs_table, two_t)
-        x1w = gather("x1w", U32, xw_table, offs_t)
+        x1w_first = sb("x1w_first", [P, HALF], U32)
+        nc.vector.tensor_copy(x1w_first[:], xw_table[:].indirect(places(offs_t, 0)))
         w1s = deal("w1s", w1s_raw, U8, 16, nc.vector)
+        xw_later = sb("xw_later", [P, HALF + N], U32, "w1s_raw")
+        x1w = [x1w_first[:], xw_later[:, :HALF]]
+        x2w = xw_later[:, HALF:]
+        nc.vector.tensor_copy(x1w[1], xw_table[:].indirect(places(offs_t, 1)))
 
-        def first_product(tag, w, ws, xw, xs):
-            banks = []
+        def product(out, w, ws, t, xw, xs):
+            rows = slice(t * P, (t + 1) * P)
+            nc.tensor.matmul_mx(out=out, lhsT=w[:, rows].bitcast(FP8X4), lhsT_scale=ws[:, rows],
+                                rhs=xw.bitcast(FP8X4), rhs_scale=xs, start=True, stop=True)
+
+        u_banks = [[psum.tile([P, 2, HALF], F32, name="bank_u%d" % (2 * h + pair)) for pair in range(2)] for h in range(2)]
+        for h in range(2):
+            cols = slice(h * HALF, (h + 1) * HALF)
             for t in range(PACK):
-                bank = psum.tile([P, N], F32, name="%s%d" % (tag, t), tag="%s%d" % (tag, t))
-                cols = slice(t * P, (t + 1) * P)
-                nc.tensor.matmul_mx(out=bank[:], lhsT=w[:, cols].bitcast(FP8X4), lhsT_scale=ws[:, cols],
-                                    rhs=xw[:].bitcast(FP8X4), rhs_scale=xs[:], start=True, stop=True)
-                banks.append(bank)
-            return banks
-
-        u_banks = first_product("bank_u", w1, w1s, x1w, x1s)
-        x2w = gather("x2w", U32, xw_table, two_t, "w1s_raw")
+                product(u_banks[h][t // 2][:, t % 2, :], w1, w1s, t, x1w[h], x1s[:, cols])
+        nc.vector.tensor_copy(x2w, xw_table[:].indirect(two_t[:]))
         w2 = deal("w2", w2_raw, I32, 4, nc.gpsimd)
         w2s = deal("w2s", w2s_raw, U8, 16, nc.gpsimd)
-        v_banks = first_product("bank_v", w2, w2s, x2w, x2s)
+        v_banks = [psum.tile([P, N], F32, name="bank_v%d" % t) for t in range(PACK)]
+        for t in range(PACK):
+            product(v_banks[t][:], w2, w2s, t, x2w, x2s[:])
 
         dw_picked = gather("dw_picked", U32, dw_table, kq_t)
         ds_picked = gather("ds_picked", U8, ds_table, kq_t)
@@ -125,9 +134,6 @@ def tile_picked_tversky2_none_po_kernel(
         eu = [[sb("eu%d%d" % (h, t), [P, HALF], F32, "ds_picked" if (h, t) == (0, ON_SCALAR) else None) for t in range(PACK)] for h in range(2)]
         tot = [sb("tot%d" % h, [P, PACK, HALF], F32, None if h else "dw_picked") for h in range(2)]
 
-        def places(lst, h):
-            return lst[:, h * HALF // 16 : (h + 1) * HALF // 16]
-
         def fetch_u(t, h):
             if t < ON_SCALAR:
                 nc.scalar.activation(eu[h][t][:], u_rows[t][:].indirect(places(la_t, h)), ACT.Exp, scale=-1.0)
@@ -137,16 +143,16 @@ def tile_picked_tversky2_none_po_kernel(
         def fetch_v(t, h):
             nc.vector.tensor_tensor(tot[h][:, t, :], ev_rows[t][:].indirect(places(lb_t, h)), eu[h][t][:], ALU.add)
 
+        for h in range(2):
+            for t in range(PACK):
+                dst, src = u_rows[t][:, h * HALF : (h + 1) * HALF], u_banks[h][t // 2][:, t % 2, :]
+                if t < ON_SCALAR:
+                    nc.scalar.activation(dst, src, ACT.Copy)
+                else:
+                    nc.scalar.activation(dst, src, ACT.Exp, scale=-1.0)
         for t in range(PACK):
-            if t < ON_SCALAR:
-                nc.scalar.activation(u_rows[t][:], u_banks[t][:], ACT.Copy)
-            else:
-                nc.scalar.activation(u_rows[t][:], u_banks[t][:], ACT.Exp, scale=-1.0)
-        for t in range(ON_SCALAR, PACK):
             fetch_u(t, 0)
         for t in range(PACK):
-            if t < ON_SCALAR:
-                fetch_u(t, 0)
             nc.scalar.activation(ev_rows[t][:], v_banks[t][:], ACT.Exp, scale=-1.0, bias=-math.log(3.0))
             fetch_v(t, 0)
         for t in range(ON_SCALAR, PACK):
@@ -175,13 +181,14 @@ def tile_picked_tversky2_none_po_kernel(
         def make_z(c):
             cols = slice(c * QUARTER, (c + 1) * QUARTER)
             root = sb("root%d" % c, [P, PACK, QUARTER], F32)
-            inv = sb("inv%d" % c, [P, PACK, QUARTER], F32)
             z_bf = sb("z_bf%d" % c, [P, QUARTER, PACK], BF16)
             nc.scalar.activation(root[:], tot[c // 2][:, :, (c % 2) * QUARTER : (c % 2 + 1) * QUARTER], ACT.Abs_reciprocal_sqrt, scale=0.75, bias=1.0)
             if c in SQUARE_ON_SCALAR:
-                nc.scalar.activation(inv[:], root[:], ACT.Square)
-                nc.vector.tensor_tensor(woven(z_bf), planes(inv), gs_t[:].unsqueeze(1).unsqueeze(3).to_broadcast([P, QUARTER // 4, PACK, 4]), ALU.mult)
+                inv = sb("inv%d" % c, [P, QUARTER, PACK], F32)
+                nc.scalar.activation(woven(inv), planes(root), ACT.Square)
+                nc.vector.tensor_tensor(z_bf[:], inv[:], gs_t[:].unsqueeze(1).to_broadcast([P, QUARTER, PACK]), ALU.mult)
             else:
+                inv = sb("inv%d" % c, [P, PACK, QUARTER], F32)
                 for t in range(PACK):
                     nc.vector.scalar_tensor_tensor(inv[:, t, :], root[:, t, :], gs_t[:, t : t + 1], root[:, t, :], ALU.mult, ALU.mult)
                 nc.vector.tensor_copy(woven(z_bf), planes(inv))

import math
from contextlib import ExitStack

import concourse.mybir as mybir

F32 = mybir.dt.float32
BF16 = mybir.dt.bfloat16
I32 = mybir.dt.int32
U32 = mybir.dt.uint32
U16 = mybir.dt.uint16
U8 = mybir.dt.uint8
FP8X4 = mybir.dt.float8_e4m3fn_x4
ACT = mybir.ActivationFunctionType
ALU = mybir.AluOpType

P = 128
PACK = 4
TABLE = 2048
N = 512
HALF = 256
QUARTER = 128
ON_SCALAR = 3
SQUARE_ON_SCALAR = (  2, 3,)
FLOPS = 3 * 2 * 512 * 512 * 512


def tile_picked_tversky2_none_po_kernel(
    tc, x_words, x_scales, w1_words, w1_scales, w2_words, w2_scales, gs, d_words, d_scales,
    offs, two, la, lb, kq, out_0, out_1, out_2,
):
    nc = tc.nc
    with ExitStack() as ctx:
        keep = ctx.enter_context(tc.tile_pool(name="keep", bufs=1))
        psum = ctx.enter_context(tc.psum_pool(name="psum", bufs=1))

        def sb(name, shape, dtype, slot=None):
            return keep.tile(shape, dtype, name=name, tag=slot or name, align_bytes=64)

        def load_list(name, src):
            tile = keep.tile([P, N // 16], U16, name=name)
            nc.sync.dma_start(tile[:], src)
            return tile

        def load_words(name, src, width, queue):
            tile = sb(name, [P, width], U32)
            queue.dma_start(tile[:].bitcast(I32), src[0].rearrange("p n t -> p (n t)").bitcast(I32))
            return tile

        def zeroed_bytes(name, width, engine):
            tile = sb(name, [P, width], U8)
            engine.memset(tile[:].bitcast(I32), 0)
            return tile

        def load_scale_rows(tile, src, quadrants, queue):
            for q in quadrants:
                queue.dma_start(tile[32 * q : 32 * q + 4, :].bitcast(I32), src[0, 4 * q : 4 * q + 4, :].bitcast(I32))

        def gather(name, dtype, table, offsets, slot=None):
            tile = sb(name, [P, N], dtype, slot)
            nc.vector.tensor_copy(tile[:], table[:].indirect(offsets[:]))
            return tile

        def deal(name, src, dtype, run, engine):
            tile = sb(name, [P, N], src.dtype)
            engine.tensor_copy(
                tile[:].bitcast(dtype).rearrange("p (t c i) -> p c t i", t=PACK, i=run),
                src[:].bitcast(dtype).rearrange("p (c i t) -> p c t i", t=PACK, i=run),
            )
            return tile

        xs_table = zeroed_bytes("xs_table", TABLE, nc.vector)
        w2s_raw = zeroed_bytes("w2s_raw", N, nc.gpsimd)
        w1s_raw = zeroed_bytes("w1s_raw", N, nc.vector)
        ds_table = zeroed_bytes("ds_table", TABLE, nc.vector)

        offs_t = load_list("offs_t", offs)
        w1_raw = load_words("w1_raw", w1_words, N, nc.sync)
        load_scale_rows(xs_table, x_scales, range(4), nc.sync)
        two_t = load_list("two_t", two)
        xw_table = load_words("xw_table", x_words, TABLE, nc.sync)
        load_scale_rows(w1s_raw, w1_scales, range(4), nc.sync)
        load_scale_rows(w2s_raw, w2_scales, range(4), nc.gpsimd)
        w2_raw = load_words("w2_raw", w2_words, N, nc.sync)
        la_t = load_list("la_t", la)
        dw_table = load_words("dw_table", d_words, TABLE, nc.sync)
        kq_t = load_list("kq_t", kq)
        for r in range(4):
            home = r if r < 2 else 14 + r
            nc.sync.dma_start(ds_table[home:P:32, :].bitcast(I32), d_scales[0, r:16:4, :].bitcast(I32))
        lb_t = load_list("lb_t", lb)
        gs_t = sb("gs_t", [P, PACK], F32)
        nc.sync.dma_start(gs_t[:], gs.rearrange("(p t) o -> p (t o)", t=PACK))

        def places(lst, h):
            return lst[:, h * HALF // 16 : (h + 1) * HALF // 16]

        w1 = deal("w1", w1_raw, I32, 4, nc.vector)
        x1s = gather("x1s", U8, xs_table, offs_t)
        x2s = gather("x2s", U8, xs_table, two_t)
        x1w_first = sb("x1w_first", [P, HALF], U32)
        nc.vector.tensor_copy(x1w_first[:], xw_table[:].indirect(places(offs_t, 0)))
        w1s = deal("w1s", w1s_raw, U8, 16, nc.vector)
        xw_later = sb("xw_later", [P, HALF + N], U32, "w1s_raw")
        x1w = [x1w_first[:], xw_later[:, :HALF]]
        x2w = xw_later[:, HALF:]
        nc.vector.tensor_copy(x1w[1], xw_table[:].indirect(places(offs_t, 1)))

        def product(out, w, ws, t, xw, xs):
            rows = slice(t * P, (t + 1) * P)
            nc.tensor.matmul_mx(out=out, lhsT=w[:, rows].bitcast(FP8X4), lhsT_scale=ws[:, rows],
                                rhs=xw.bitcast(FP8X4), rhs_scale=xs, start=True, stop=True)

        u_banks = [[psum.tile([P, 2, HALF], F32, name="bank_u%d" % (2 * h + pair)) for pair in range(2)] for h in range(2)]
        for h in range(2):
            cols = slice(h * HALF, (h + 1) * HALF)
            for t in range(PACK):
                product(u_banks[h][t // 2][:, t % 2, :], w1, w1s, t, x1w[h], x1s[:, cols])
        nc.vector.tensor_copy(x2w, xw_table[:].indirect(two_t[:]))
        w2 = deal("w2", w2_raw, I32, 4, nc.gpsimd)
        w2s = deal("w2s", w2s_raw, U8, 16, nc.gpsimd)
        v_banks = [psum.tile([P, N], F32, name="bank_v%d" % t) for t in range(PACK)]
        for t in range(PACK):
            product(v_banks[t][:], w2, w2s, t, x2w, x2s[:])

        dw_picked = gather("dw_picked", U32, dw_table, kq_t)
        ds_picked = gather("ds_picked", U8, ds_table, kq_t)
        dw = deal("dw", dw_picked, I32, 4, nc.vector)
        ds = deal("ds", ds_picked, U8, 16, nc.vector)
        for r in (2, 3):
            nc.sync.dma_start(ds[r:P:32, :].bitcast(I32), ds[14 + r:P:32, :].bitcast(I32))

        u_rows = [sb("u_rows%d" % t, [P, N], F32) for t in range(PACK)]
        ev_rows = [sb("ev_rows%d" % t, [P, N], F32) for t in range(PACK)]
        eu = [[sb("eu%d%d" % (h, t), [P, HALF], F32, "ds_picked" if (h, t) == (0, ON_SCALAR) else None) for t in range(PACK)] for h in range(2)]
        tot = [sb("tot%d" % h, [P, PACK, HALF], F32, None if h else "dw_picked") for h in range(2)]

        def fetch_u(t, h):
            if t < ON_SCALAR:
                nc.scalar.activation(eu[h][t][:], u_rows[t][:].indirect(places(la_t, h)), ACT.Exp, scale=-1.0)
            else:
                nc.vector.tensor_copy(eu[h][t][:], u_rows[t][:].indirect(places(la_t, h)))

        def fetch_v(t, h):
            nc.vector.tensor_tensor(tot[h][:, t, :], ev_rows[t][:].indirect(places(lb_t, h)), eu[h][t][:], ALU.add)

        for h in range(2):
            for t in range(PACK):
                dst, src = u_rows[t][:, h * HALF : (h + 1) * HALF], u_banks[h][t // 2][:, t % 2, :]
                if t < ON_SCALAR:
                    nc.scalar.activation(dst, src, ACT.Copy)
                else:
                    nc.scalar.activation(dst, src, ACT.Exp, scale=-1.0)
        for t in range(PACK):
            fetch_u(t, 0)
        for t in range(PACK):
            nc.scalar.activation(ev_rows[t][:], v_banks[t][:], ACT.Exp, scale=-1.0, bias=-math.log(3.0))
            fetch_v(t, 0)
        for t in range(ON_SCALAR, PACK):
            fetch_u(t, 1)
        for t in range(PACK):
            if t < ON_SCALAR:
                fetch_u(t, 1)
            fetch_v(t, 1)

        z_words = sb("z_words", [P, N], U32)
        z_scales = sb("z_scales", [P, N], U8)
        y_words = sb("y_words", [P, N], U32)
        y_scales = sb("y_scales", [P, N], U8)
        out_rows = out_0.rearrange("(p t) j -> p t j", t=PACK)
        words_out = out_1[0].rearrange("p n t -> p (n t)").bitcast(I32)

        def woven(tile):
            return tile[:].rearrange("p (c i) t -> p c t i", i=4)

        def planes(tile):
            return tile[:].rearrange("p t (c i) -> p c t i", i=4)

        def flat(tile):
            return tile[:].rearrange("p j t -> p (j t)")

        def make_z(c):
            cols = slice(c * QUARTER, (c + 1) * QUARTER)
            root = sb("root%d" % c, [P, PACK, QUARTER], F32)
            z_bf = sb("z_bf%d" % c, [P, QUARTER, PACK], BF16)
            nc.scalar.activation(root[:], tot[c // 2][:, :, (c % 2) * QUARTER : (c % 2 + 1) * QUARTER], ACT.Abs_reciprocal_sqrt, scale=0.75, bias=1.0)
            if c in SQUARE_ON_SCALAR:
                inv = sb("inv%d" % c, [P, QUARTER, PACK], F32)
                nc.scalar.activation(woven(inv), planes(root), ACT.Square)
                nc.vector.tensor_tensor(z_bf[:], inv[:], gs_t[:].unsqueeze(1).to_broadcast([P, QUARTER, PACK]), ALU.mult)
            else:
                inv = sb("inv%d" % c, [P, PACK, QUARTER], F32)
                for t in range(PACK):
                    nc.vector.scalar_tensor_tensor(inv[:, t, :], root[:, t, :], gs_t[:, t : t + 1], root[:, t, :], ALU.mult, ALU.mult)
                nc.vector.tensor_copy(woven(z_bf), planes(inv))
            nc.vector.quantize_mx(z_words[:, cols].bitcast(FP8X4), z_scales[:, cols], flat(z_bf))

        def make_y(c):
            cols = slice(c * QUARTER, (c + 1) * QUARTER)
            y = sb("y%d" % c, [P, PACK, QUARTER], F32)
            y_bf = sb("y_bf%d" % c, [P, QUARTER, PACK], BF16)
            bank = psum.tile([P, PACK, QUARTER], F32, name="bank_y%d" % c, tag="bank_u%d" % c)
            for t in range(PACK):
                rows = slice(t * P, (t + 1) * P)
                nc.tensor.matmul_mx(out=bank[:, t, :], lhsT=dw[:, rows].bitcast(FP8X4), lhsT_scale=ds[:, rows],
                                    rhs=z_words[:, cols].bitcast(FP8X4), rhs_scale=z_scales[:, cols], start=True, stop=True)
            nc.scalar.activation(y[:], bank[:], ACT.Copy, scale=0.0625)
            nc.sync.dma_start(out_rows[:, :, cols], y[:])
            nc.vector.tensor_copy(woven(y_bf), planes(y))
            nc.vector.quantize_mx(y_words[:, cols].bitcast(FP8X4), y_scales[:, cols], flat(y_bf))

        for c in range(4):
            make_z(c)
        for c in range(4):
            make_y(c)
            if c == 1:
                nc.sync.dma_start(words_out[:, :HALF], y_words[:, :HALF].bitcast(I32))
        nc.sync.dma_start(words_out[:, HALF:], y_words[:, HALF:].bitcast(I32))
        for q in range(4):
            queue = nc.sync if q % 2 else nc.scalar
            queue.dma_start(out_2[0, 4 * q : 4 * q + 4, :].bitcast(I32), y_scales[32 * q : 32 * q + 4, :].bitcast(I32))
